import numpy as np
import ml_dtypes


def mxq(x, axis, fmt="e4m3"):
    dtype, down = {"e4m3": (ml_dtypes.float8_e4m3fn, 7), "e5m2": (ml_dtypes.float8_e5m2, 14)}[fmt]
    v = np.moveaxis(np.asarray(x, np.float32).astype(ml_dtypes.bfloat16).astype(np.float64), axis, -1)
    blocks = v.reshape(v.shape[:-1] + (-1, 32))
    amax = np.abs(blocks).max(-1, keepdims=True)
    byte = np.maximum(np.where(amax > 0, np.frexp(amax)[1] - 1 + 127, 0) - down, 1)
    scale = np.exp2(byte - 127.0)
    codes = (blocks / scale).astype(np.float32).astype(dtype).astype(np.float64)
    return np.moveaxis((codes * scale).reshape(v.shape), -1, axis)


WIDE = False


def mx_kscale(k):
    if not WIDE:
        return np.ones(k)
    levels = np.array([10, -10, 5, -5, 0])
    if k % 512:
        return np.exp2(np.random.permutation(np.resize(levels, k // 32))).repeat(32)
    a = np.empty((k // 512, 16))
    for p in range(k // 512):
        a[p, :8] = np.random.permutation(np.resize(levels, 8))
        for g in range(8):
            far = levels[np.abs(levels - a[p, g]) >= 10]
            a[p, g + 8] = far[np.random.randint(len(far))]
    return np.exp2(a.ravel()).repeat(32)


BF16 = ml_dtypes.bfloat16


def bf(x):
    return np.asarray(x, np.float32).astype(BF16)


def f64(x):
    return np.asarray(x).astype(np.float64)


B, N, CQ, CK = 2, 512, 512, 512

EPS = 1e-6


def channel_map(q, k, temp):
    n = q.shape[1]
    gram = mxq(q, 1, "e4m3").transpose(0, 2, 1) @ mxq(k, 1, "e4m3")
    a = temp[None, :, None] * gram / np.sqrt(n)
    e = np.exp(a - a.max(axis=-1, keepdims=True))
    return e / e.sum(axis=-1, keepdims=True)


def rms_normalize(o):
    return o / np.sqrt(np.mean(o * o, axis=-1, keepdims=True) + EPS)


def draw0():
    s, t = mx_kscale(N), mx_kscale(CK)
    return {
        "q": bf(np.random.standard_normal((B, N, CQ)) * s[None, :, None]),
        "k": bf(np.random.standard_normal((B, N, CK)) / s[None, :, None]),
        "v": bf(np.random.standard_normal((B, N, CK)) * 0.03 * t[None, None, :]),
        "temp": bf(1.0 + 0.1 * np.random.standard_normal(CQ)),
        "u": bf(np.random.standard_normal(CK) * 0.03 * np.sqrt(CK / CQ) / t),
        "zs": bf(np.random.standard_normal((B, CQ)) * 0.5),
        "zb": bf(np.random.standard_normal((B, CQ)) * 0.5),
    }


def core(q, k, v, temp, u, zs, zb):
    q, k, v = f64(q), f64(k), f64(v)
    temp, u, zs, zb = f64(temp), f64(u), f64(zs), f64(zb)
    c = q.shape[2]
    p = channel_map(q, k, temp)
    pu = p * u[None, None, :] * np.sqrt(c)
    o = mxq(v, 2, "e4m3") @ mxq(pu, 2, "e4m3").transpose(0, 2, 1)
    on = rms_normalize(o)
    return on * (1.0 + zs[:, None, :]) + zb[:, None, :]


def e4m3fn_bytes(y):
    return np.clip(np.asarray(y, np.float64), -448.0, 448.0).astype(np.float32).astype(ml_dtypes.float8_e4m3fn).view(np.uint8)


def e4m3fn_values(b):
    return np.asarray(b, np.uint8).view(ml_dtypes.float8_e4m3fn).astype(np.float64)


def setup_inputs():
    d = draw0()
    x0 = np.asarray(d['v']).astype(np.float64)
    s = (np.max(np.abs(x0), axis=(0, 1), keepdims=True) / 448.0).astype(np.float32)
    out = {}
    for k, v in d.items():
        if k == 'v':
            out['v_bytes'] = e4m3fn_bytes(x0 / s.astype(np.float64))
            out['v_scale'] = s
        else:
            out[k] = v
    return out


def reference(q, k, v_bytes, v_scale, temp, u, zs, zb):
    return core(q, k, e4m3fn_values(v_bytes) * v_scale.astype(np.float64), temp, u, zs, zb)

@@ -1,0 +1,393 @@
+import math
+from contextlib import ExitStack
+
+import concourse.mybir as mybir
+from concourse.masks import make_identity
+
+B, N, C = 2, 512, 512
+EPS = 1e-6
+FLOPS = 2 * B * (N * C * C + N * C * C)
+
+F32 = mybir.dt.float32
+BF16 = mybir.dt.bfloat16
+U32 = mybir.dt.uint32
+U8 = mybir.dt.uint8
+FP8 = mybir.dt.float8_e4m3fn
+FP8X4 = mybir.dt.float8_e4m3fn_x4
+ALU = mybir.AluOpType
+ACT = mybir.ActivationFunctionType
+
+P = 128
+PACK = 4
+TILES = 4
+HALF = C // 2
+
+
+def tile_diffirpriorchannelattention_kernel(tc, q, k, v_bytes, v_scale, temp, u, zs, zb, out):
+    nc = tc.nc
+    with ExitStack() as ctx:
+        sb = ctx.enter_context(tc.tile_pool(name="sb", bufs=1))
+        psum = ctx.enter_context(tc.psum_pool(name="psum", bufs=1))
+        ctx.enter_context(tc.manual_schedule())
+
+        def bank(number, shape, dtype, name):
+            return psum.tile(shape, dtype, name=name, tag="bank%d" % number)
+
+        def per_sample(stem, shape, dtype):
+            return [sb.tile(shape, dtype, name="%s%d" % (stem, b), align_bytes=64) for b in range(B)]
+
+        def per_part(stem, parts, shape, dtype):
+            return [
+                [sb.tile(shape, dtype, name="%s%d_%d" % (stem, b, t), align_bytes=64) for t in range(parts)]
+                for b in range(B)
+            ]
+
+        q_raw = per_sample("q_raw", [P, PACK, C], BF16)
+        k_raw = per_sample("k_raw", [P, PACK, C], BF16)
+        v_raw = per_sample("v_raw", [P, TILES, C], U8)
+        staged = [sb.tile([P, HALF, PACK], BF16, name="staged%d" % s, align_bytes=64) for s in range(5)]
+        k_grouped = [[staged[0], staged[1]], [staged[3], staged[2]]]
+        q_grouped = [[staged[2], staged[3]], [staged[0], staged[4]]]
+        v_grouped = per_part("v_grouped", 2, [P, HALF, PACK], BF16)
+        pu_grouped = per_part("pu_grouped", 2, [P, HALF, PACK], BF16)
+        codes = {name: per_sample(name + "_codes", [P, C], U32) for name in ("q", "k", "v", "pu")}
+        scales = {name: per_sample(name + "_scales", [P, C], U8) for name in ("q", "k", "v", "pu")}
+        grouped = {"q": q_grouped, "k": k_grouped, "v": v_grouped, "pu": pu_grouped}
+        raw = {"q": q_raw, "k": k_raw}
+        v_wide = per_part("v_wide", TILES, [P, C], BF16)
+        neg_a = per_part("neg_a", TILES, [P, C], F32)
+        e = per_part("e", TILES, [P, C], F32)
+        pu = per_part("pu", TILES, [P, C], BF16)
+        gained = per_part("gained", TILES, [P, C], F32)
+        result = per_part("result", TILES, [P, C], F32)
+        neg_max = per_sample("neg_max", [P, TILES], F32)
+        e_sum = per_sample("e_sum", [P, TILES], F32)
+        inv_sum = per_sample("inv_sum", [P, TILES], F32)
+        mean_sq = per_sample("mean_sq", [P, TILES], F32)
+        rms = per_sample("rms", [P, TILES], F32)
+        inv_rms = per_sample("inv_rms", [P, TILES], F32)
+        gain = per_sample("gain", [P, C], F32)
+        shift = sb.tile([P, B, C], BF16, name="shift")
+        squares = sb.tile([P, C], BF16, name="squares")
+        rows = sb.tile([P, P], BF16, name="rows")
+        ident32 = sb.tile([P, P], F32, name="ident32")
+        ident16 = sb.tile([P, P], BF16, name="ident16")
+        vs_cols = sb.tile([P, PACK], F32, name="vs_cols")
+        vs_all = sb.tile([P, C], F32, name="vs_all")
+        neg_temp = sb.tile([P, TILES], F32, name="neg_temp")
+        u_cols = sb.tile([P, TILES], F32, name="u_cols")
+        gain_cols = sb.tile([P, B * TILES], F32, name="gain_cols")
+
+        shift_cols = sb.tile([P, B * TILES], F32, name="shift_cols")
+        minus_half = sb.tile([P, TILES], F32, name="minus_half")
+        warm = sb.tile([P, 2], F32, name="warm")
+        nc.vector.memset(rows[:], 0.0)
+        nc.vector.memset(warm[:, 0:1], 0.0)
+        make_identity(nc, ident32[:])
+        nc.vector.memset(minus_half[:], -0.5)
+        nc.vector.tensor_copy(out=ident16[:], in_=ident32[:])
+
+        def load_tokens(name, source, b):
+            nc.sync.dma_start(out=raw[name][b][:], in_=source[b].rearrange("(p j) c -> p j c", j=PACK))
+
+        def load_v(b):
+            nc.sync.dma_start(out=v_raw[b][:], in_=v_bytes[b].rearrange("(p m) c -> p m c", m=TILES))
+
+        nc.scalar.dma_start(out=vs_cols[:], in_=v_scale.rearrange("a b (p t) -> p (a b t)", t=PACK))
+        nc.scalar.dma_start(out=rows[0:4, :], in_=temp.rearrange("(t p) -> t p", p=P))
+        nc.scalar.dma_start(out=rows[4:8, :], in_=u.rearrange("(t p) -> t p", p=P))
+        nc.scalar.dma_start(out=rows[8:16, :], in_=zs.rearrange("b (t p) -> (b t) p", p=P))
+        nc.scalar.dma_start(out=rows[16:24, :], in_=zb.rearrange("b (t p) -> (b t) p", p=P))
+        nc.scalar.activation(out=warm[:, 1:2], in_=warm[:, 0:1], func=ACT.Exp)
+        load_tokens("k", k, 0)
+        load_v(0)
+        load_tokens("q", q, 0)
+        load_v(1)
+        load_tokens("k", k, 1)
+        load_tokens("q", q, 1)
+        nc.sync.dma_start(
+            out=shift[:].rearrange("p b c -> p (b c)"),
+            in_=zb.rearrange("b c -> (b c)").partition_broadcast(P),
+        )
+
+        vs_bank = bank(2, [P, C], F32, "vs_bank")
+        for t in range(PACK):
+            nc.tensor.transpose(vs_bank[:, t::PACK], vs_cols[:, t : t + 1].to_broadcast([P, P]), ident32[:])
+        nc.scalar.copy(out=vs_all[:], in_=vs_bank[:])
+
+        cols_bank = bank(1, [P, P], BF16, "cols_bank")
+        nc.tensor.transpose(cols_bank[:], rows[:], ident16[:])
+        nc.scalar.activation(out=u_cols[:], in_=cols_bank[:, 4:8], func=ACT.Copy, scale=math.sqrt(C))
+        nc.scalar.activation(out=gain_cols[:], in_=cols_bank[:, 8:16], func=ACT.Copy, bias=1.0)
+        nc.scalar.activation(out=neg_temp[:], in_=cols_bank[:, 0:4], func=ACT.Copy, scale=-1.0 / math.sqrt(N))
+
+        nc.scalar.activation(out=shift_cols[:], in_=cols_bank[:, 16:24], func=ACT.Copy)
+
+        def spread(target, cols, first):
+            for t in range(TILES):
+                column = cols[:, first + t : first + t + 1]
+                nc.tensor.transpose(target[:, t * P : (t + 1) * P], column.to_broadcast([P, P]), ident32[:])
+
+        gain_banks = [bank(6 + b, [P, C], F32, "gain_bank%d" % b) for b in range(B)]
+        for b in range(B):
+            spread(gain_banks[b], gain_cols, b * TILES)
+        u_bank = bank(0, [P, C], F32, "u_bank")
+        spread(u_bank, u_cols, 0)
+
+        gram_banks, o_banks, turn_banks, shift_banks = {}, {}, {}, {}
+
+        def keep_gain(b):
+            nc.scalar.copy(out=gain[b][:], in_=gain_banks[b][:])
+
+        def interleave(name, b, h, engine):
+            source = raw[name][b][:, :, h * HALF : (h + 1) * HALF].rearrange("p j c -> p c j")
+            if engine == "vector":
+                nc.vector.tensor_copy(out=grouped[name][b][h][:], in_=source)
+            elif engine == "scalar":
+                nc.scalar.copy(out=grouped[name][b][h][:], in_=source)
+            else:
+                nc.gpsimd.tensor_scalar(
+                    out=grouped[name][b][h][:], in0=source, scalar1=1.0, scalar2=0.0, op0=ALU.mult, op1=ALU.add
+                )
+
+        def quantize(name, b, h):
+            cols = slice(h * HALF, (h + 1) * HALF)
+            nc.vector.quantize_mx(
+                out=codes[name][b][:, cols].bitcast(FP8X4),
+                scales=scales[name][b][:, cols],
+                in_=grouped[name][b][h][:].rearrange("p c j -> p (c j)"),
+            )
+
+        def product(target, left, right, b, t):
+            cols = slice(t * P, (t + 1) * P)
+            nc.tensor.matmul_mx(
+                out=target[:],
+                lhsT=codes[left][b][:, cols].bitcast(FP8X4),
+                lhsT_scale=scales[left][b][:, cols],
+                rhs=codes[right][b][:].bitcast(FP8X4),
+                rhs_scale=scales[right][b][:],
+                start=True,
+                stop=True,
+            )
+
+        def gram(b, t, number):
+            gram_banks[b, t] = bank(number, [P, C], F32, "gram%d_%d" % (b, t))
+            product(gram_banks[b, t], "q", "k", b, t)
+
+        def row_max(b, t):
+            nc.vector.tensor_scalar(
+                out=neg_a[b][t][:], in0=gram_banks[b, t][:], scalar1=neg_temp[:, t : t + 1], scalar2=None,
+                op0=ALU.mult, op1=ALU.min, accum_out=neg_max[b][:, t : t + 1],
+            )
+
+        def exponential(b, t):
+            nc.scalar.activation(
+                out=e[b][t][:], in_=neg_a[b][t][:], func=ACT.Exp, scale=-1.0,
+                bias=neg_max[b][:, t : t + 1], accum_out=e_sum[b][:, t : t + 1],
+            )
+
+        def invert_sum(b, first, last):
+            nc.vector.reciprocal(out=inv_sum[b][:, first:last], in_=e_sum[b][:, first:last])
+
+        def weigh(b, t):
+            nc.vector.scalar_tensor_tensor(
+                out=pu[b][t][:], in0=e[b][t][:], scalar=inv_sum[b][:, t : t + 1], in1=u_bank[:],
+                op0=ALU.mult, op1=ALU.mult,
+            )
+
+        def scale_v(b, t):
+            nc.vector.tensor_tensor(out=v_wide[b][t][:], in0=v_raw[b][:, t, :].bitcast(FP8), in1=vs_all[:], op=ALU.mult)
+
+        def turn(name, source, b, h, number):
+            turn_banks[name, b, h] = bank(number, [P, 2, 2, P], F32, "turn_%s%d_%d" % (name, b, h))
+            for s in range(2):
+                words = source[b][2 * h + s][:].bitcast(F32)
+                for w in range(2):
+                    nc.tensor.transpose(turn_banks[name, b, h][:, s, w, :], words[:, w::2], ident32[:])
+
+        def keep_turn(name, b, h):
+            target = grouped[name][b][h][:].rearrange("p c j -> p (c j)").bitcast(F32)
+            nc.scalar.copy(
+                out=target.rearrange("p (s r w) -> p s r w", s=2, w=2),
+                in_=turn_banks[name, b, h][:].rearrange("p s w r -> p s r w"),
+            )
+
+        def mix(b, t, number):
+            o_banks[b, t] = bank(number, [P, C], F32, "o%d_%d" % (b, t))
+            product(o_banks[b, t], "v", "pu", b, t)
+
+        def square(b, t):
+            nc.scalar.activation(
+                out=squares[:], in_=o_banks[b, t][:], func=ACT.Square, scale=1.0 / math.sqrt(C),
+                accum_out=mean_sq[b][:, t : t + 1],
+            )
+
+        def root(b, first, last):
+            nc.scalar.activation(out=rms[b][:, first:last], in_=mean_sq[b][:, first:last], func=ACT.Sqrt, bias=EPS)
+
+        def power(b, first, last):
+            nc.gpsimd.tensor_scalar(
+                out=rms[b][:, first:last], in0=mean_sq[b][:, first:last], scalar1=EPS, scalar2=1.0,
+                op0=ALU.add, op1=ALU.mult,
+            )
+            nc.gpsimd.tensor_tensor(
+                out=inv_rms[b][:, first:last], in0=rms[b][:, first:last], in1=minus_half[:, first:last], op=ALU.pow
+            )
+
+        def invert_rms(b, first, last):
+            nc.vector.reciprocal(out=inv_rms[b][:, first:last], in_=rms[b][:, first:last])
+
+        def normalize(b, t):
+            nc.vector.scalar_tensor_tensor(
+                out=gained[b][t][:], in0=o_banks[b, t][:], scalar=inv_rms[b][:, t : t + 1], in1=gain[b][:],
+                op0=ALU.mult, op1=ALU.mult,
+            )
+
+        def spread_shift(b, number):
+            shift_banks[b] = bank(number, [P, C], F32, "shift_bank%d" % b)
+            spread(shift_banks[b], shift_cols, b * TILES)
+
+        def finish(b, t, on_gpsimd):
+            if on_gpsimd is None:
+                nc.vector.tensor_tensor(out=result[b][t][:], in0=gained[b][t][:], in1=shift[:, b, :], op=ALU.add)
+            elif on_gpsimd:
+                nc.gpsimd.tensor_tensor(out=result[b][t][:], in0=gained[b][t][:], in1=shift[:, b, :], op=ALU.add)
+            else:
+                nc.vector.tensor_tensor(out=result[b][t][:], in0=gained[b][t][:], in1=shift_banks[b][:], op=ALU.add)
+            nc.sync.dma_start(out=out[b].rearrange("(p m) c -> p m c", m=TILES)[:, t, :], in_=result[b][t][:])
+
+        interleave("k", 0, 0, "vector")
+        interleave("k", 0, 1, "scalar")
+        quantize("k", 0, 0)
+        scale_v(0, 0)
+        scale_v(0, 1)
+        turn("v", v_wide, 0, 0, 4)
+        interleave("q", 0, 0, "scalar")
+        scale_v(0, 2)
+        scale_v(0, 3)
+        turn("v", v_wide, 0, 1, 5)
+        quantize("k", 0, 1)
+        quantize("q", 0, 0)
+        gram(0, 0, 1)
+        gram(0, 1, 2)
+        interleave("q", 0, 1, "scalar")
+        keep_gain(0)
+        keep_gain(1)
+        keep_turn("v", 0, 0)
+        scale_v(1, 0)
+        scale_v(1, 1)
+        quantize("q", 0, 1)
+        gram(0, 2, 3)
+        interleave("k", 1, 0, "gpsimd")
+        interleave("k", 1, 1, "gpsimd")
+        interleave("q", 1, 0, "gpsimd")
+        row_max(0, 0)
+        gram(0, 3, 1)
+        turn("v", v_wide, 1, 0, 4)
+        exponential(0, 0)
+        row_max(0, 1)
+        exponential(0, 1)
+        row_max(0, 2)
+        exponential(0, 2)
+        invert_sum(0, 0, 1)
+        row_max(0, 3)
+        exponential(0, 3)
+        invert_sum(0, 1, 2)
+        weigh(0, 0)
+        invert_sum(0, 2, 3)
+        weigh(0, 1)
+        turn("pu", pu, 0, 0, 2)
+        invert_sum(0, 3, 4)
+        weigh(0, 2)
+        weigh(0, 3)
+        turn("pu", pu, 0, 1, 3)
+        interleave("q", 1, 1, "scalar")
+        keep_turn("pu", 0, 0)
+        keep_turn("v", 0, 1)
+        keep_turn("pu", 0, 1)
+        keep_turn("v", 1, 0)
+        quantize("k", 1, 0)
+        quantize("k", 1, 1)
+        quantize("q", 1, 0)
+        gram(1, 0, 6)
+        gram(1, 1, 7)
+        quantize("v", 0, 0)
+        quantize("pu", 0, 0)
+        quantize("q", 1, 1)
+        gram(1, 2, 1)
+        quantize("v", 0, 1)
+        quantize("pu", 0, 1)
+        mix(0, 0, 2)
+        mix(0, 1, 3)
+        scale_v(1, 2)
+        scale_v(1, 3)
+        square(0, 0)
+        row_max(1, 0)
+        gram(1, 3, 6)
+        mix(0, 2, 4)
+        mix(0, 3, 5)
+        exponential(1, 0)
+        row_max(1, 1)
+        turn("v", v_wide, 1, 1, 7)
+        exponential(1, 1)
+        row_max(1, 2)
+        exponential(1, 2)
+        invert_sum(1, 0, 1)
+        row_max(1, 3)
+        exponential(1, 3)
+        square(0, 1)
+        power(0, 0, 2)
+        invert_sum(1, 1, 2)
+        weigh(1, 0)
+        invert_sum(1, 2, 3)
+        weigh(1, 1)
+        turn("pu", pu, 1, 0, 6)
+        square(0, 2)
+        power(0, 2, 3)
+        square(0, 3)
+        keep_turn("pu", 1, 0)
+        keep_turn("v", 1, 1)
+        invert_sum(1, 3, 4)
+        weigh(1, 2)
+        weigh(1, 3)
+        turn("pu", pu, 1, 1, 1)
+        keep_turn("pu", 1, 1)
+        root(0, 3, 4)
+        quantize("v", 1, 0)
+        quantize("pu", 1, 0)
+        normalize(0, 0)
+        spread_shift(0, 2)
+        quantize("v", 1, 1)
+        quantize("pu", 1, 1)
+        mix(1, 0, 7)
+        mix(1, 1, 0)
+        mix(1, 2, 6)
+        mix(1, 3, 1)
+        normalize(0, 1)
+        finish(0, 1, True)
+        spread_shift(1, 3)
+        normalize(0, 2)
+        invert_rms(0, 3, 4)
+        finish(0, 0, False)
+        finish(0, 2, True)
+        normalize(0, 3)
+        square(1, 0)
+        square(1, 1)
+        root(1, 0, 1)
+        square(1, 2)
+        root(1, 1, 2)
+        square(1, 3)
+        root(1, 2, 3)
+        root(1, 3, 4)
+        invert_rms(1, 0, 1)
+        finish(0, 3, False)
+        invert_rms(1, 1, 2)
+        normalize(1, 0)
+        finish(1, 0, True)
+        normalize(1, 1)
+        invert_rms(1, 2, 4)
+        finish(1, 1, False)
+        normalize(1, 2)
+        normalize(1, 3)
+        finish(1, 2, False)
+        finish(1, 3, False)

@@ -21,6 +21,7 @@ P = 128
 PACK = 4
 TILES = 4
 HALF = C // 2
+RUN = 4
 
 
 def tile_diffirpriorchannelattention_kernel(tc, q, k, v_bytes, v_scale, temp, u, zs, zb, out):
@@ -45,11 +46,11 @@ def tile_diffirpriorchannelattention_kernel(tc, q, k, v_bytes, v_scale, temp, u,
         q_raw = per_sample("q_raw", [P, PACK, C], BF16)
         k_raw = per_sample("k_raw", [P, PACK, C], BF16)
         v_raw = per_sample("v_raw", [P, TILES, C], U8)
-        staged = [sb.tile([P, HALF, PACK], BF16, name="staged%d" % s, align_bytes=64) for s in range(5)]
-        k_grouped = [[staged[0], staged[1]], [staged[3], staged[2]]]
-        q_grouped = [[staged[2], staged[3]], [staged[0], staged[4]]]
-        v_grouped = per_part("v_grouped", 2, [P, HALF, PACK], BF16)
-        pu_grouped = per_part("pu_grouped", 2, [P, HALF, PACK], BF16)
+        staged = [sb.tile([P, C * PACK], BF16, name="staged%d" % s, align_bytes=64) for s in range(2)]
+        k_grouped = [staged[0], staged[1]]
+        q_grouped = [staged[1], staged[0]]
+        v_grouped = per_sample("v_grouped", [P, C * PACK], BF16)
+        pu_grouped = per_sample("pu_grouped", [P, C * PACK], BF16)
         codes = {name: per_sample(name + "_codes", [P, C], U32) for name in ("q", "k", "v", "pu")}
         scales = {name: per_sample(name + "_scales", [P, C], U8) for name in ("q", "k", "v", "pu")}
         grouped = {"q": q_grouped, "k": k_grouped, "v": v_grouped, "pu": pu_grouped}
@@ -79,12 +80,10 @@ def tile_diffirpriorchannelattention_kernel(tc, q, k, v_bytes, v_scale, temp, u,
         gain_cols = sb.tile([P, B * TILES], F32, name="gain_cols")
 
         shift_cols = sb.tile([P, B * TILES], F32, name="shift_cols")
-        minus_half = sb.tile([P, TILES], F32, name="minus_half")
         warm = sb.tile([P, 2], F32, name="warm")
         nc.vector.memset(rows[:], 0.0)
         nc.vector.memset(warm[:, 0:1], 0.0)
         make_identity(nc, ident32[:])
-        nc.vector.memset(minus_half[:], -0.5)
         nc.vector.tensor_copy(out=ident16[:], in_=ident32[:])
 
         def load_tokens(name, source, b):
@@ -93,7 +92,7 @@ def tile_diffirpriorchannelattention_kernel(tc, q, k, v_bytes, v_scale, temp, u,
         def load_v(b):
             nc.sync.dma_start(out=v_raw[b][:], in_=v_bytes[b].rearrange("(p m) c -> p m c", m=TILES))
 
-        nc.scalar.dma_start(out=vs_cols[:], in_=v_scale.rearrange("a b (p t) -> p (a b t)", t=PACK))
+        nc.sync.dma_start(out=vs_cols[:], in_=v_scale.rearrange("a b (p t) -> p (a b t)", t=PACK))
         nc.scalar.dma_start(out=rows[0:4, :], in_=temp.rearrange("(t p) -> t p", p=P))
         nc.scalar.dma_start(out=rows[4:8, :], in_=u.rearrange("(t p) -> t p", p=P))
         nc.scalar.dma_start(out=rows[8:16, :], in_=zs.rearrange("b (t p) -> (b t) p", p=P))
@@ -140,22 +139,22 @@ def tile_diffirpriorchannelattention_kernel(tc, q, k, v_bytes, v_scale, temp, u,
             nc.scalar.copy(out=gain[b][:], in_=gain_banks[b][:])
 
         def interleave(name, b, h, engine):
-            source = raw[name][b][:, :, h * HALF : (h + 1) * HALF].rearrange("p j c -> p c j")
+            source = raw[name][b][:, :, h * HALF : (h + 1) * HALF].rearrange("p j (c i) -> p c j i", i=RUN)
+            target = grouped[name][b][:, h * HALF * PACK : (h + 1) * HALF * PACK]
+            target = target.rearrange("p (c i j) -> p c j i", i=RUN, j=PACK)
             if engine == "vector":
-                nc.vector.tensor_copy(out=grouped[name][b][h][:], in_=source)
+                nc.vector.tensor_copy(out=target, in_=source)
             elif engine == "scalar":
-                nc.scalar.copy(out=grouped[name][b][h][:], in_=source)
+                nc.scalar.copy(out=target, in_=source)
             else:
-                nc.gpsimd.tensor_scalar(
-                    out=grouped[name][b][h][:], in0=source, scalar1=1.0, scalar2=0.0, op0=ALU.mult, op1=ALU.add
-                )
+                nc.gpsimd.tensor_scalar(out=target, in0=source, scalar1=1.0, scalar2=0.0, op0=ALU.mult, op1=ALU.add)
 
-        def quantize(name, b, h):
-            cols = slice(h * HALF, (h + 1) * HALF)
+        def quantize(name, b, first, last):
+            cols = slice(first * HALF, last * HALF)
             nc.vector.quantize_mx(
                 out=codes[name][b][:, cols].bitcast(FP8X4),
                 scales=scales[name][b][:, cols],
-                in_=grouped[name][b][h][:].rearrange("p c j -> p (c j)"),
+                in_=grouped[name][b][:, first * HALF * PACK : last * HALF * PACK],
             )
 
         def product(target, left, right, b, t):
@@ -206,7 +205,7 @@ def tile_diffirpriorchannelattention_kernel(tc, q, k, v_bytes, v_scale, temp, u,
                     nc.tensor.transpose(turn_banks[name, b, h][:, s, w, :], words[:, w::2], ident32[:])
 
         def keep_turn(name, b, h):
-            target = grouped[name][b][h][:].rearrange("p c j -> p (c j)").bitcast(F32)
+            target = grouped[name][b][:, h * HALF * PACK : (h + 1) * HALF * PACK].bitcast(F32)
             nc.scalar.copy(
                 out=target.rearrange("p (s r w) -> p s r w", s=2, w=2),
                 in_=turn_banks[name, b, h][:].rearrange("p s w r -> p s r w"),
@@ -224,15 +223,6 @@ def tile_diffirpriorchannelattention_kernel(tc, q, k, v_bytes, v_scale, temp, u,
 
         def root(b, first, last):
             nc.scalar.activation(out=rms[b][:, first:last], in_=mean_sq[b][:, first:last], func=ACT.Sqrt, bias=EPS)
-
-        def power(b, first, last):
-            nc.gpsimd.tensor_scalar(
-                out=rms[b][:, first:last], in0=mean_sq[b][:, first:last], scalar1=EPS, scalar2=1.0,
-                op0=ALU.add, op1=ALU.mult,
-            )
-            nc.gpsimd.tensor_tensor(
-                out=inv_rms[b][:, first:last], in0=rms[b][:, first:last], in1=minus_half[:, first:last], op=ALU.pow
-            )
 
         def invert_rms(b, first, last):
             nc.vector.reciprocal(out=inv_rms[b][:, first:last], in_=rms[b][:, first:last])
@@ -258,16 +248,15 @@ def tile_diffirpriorchannelattention_kernel(tc, q, k, v_bytes, v_scale, temp, u,
 
         interleave("k", 0, 0, "vector")
         interleave("k", 0, 1, "scalar")
-        quantize("k", 0, 0)
         scale_v(0, 0)
         scale_v(0, 1)
         turn("v", v_wide, 0, 0, 4)
         interleave("q", 0, 0, "scalar")
         scale_v(0, 2)
+        quantize("k", 0, 0, 2)
         scale_v(0, 3)
         turn("v", v_wide, 0, 1, 5)
-        quantize("k", 0, 1)
-        quantize("q", 0, 0)
+        quantize("q", 0, 0, 1)
         gram(0, 0, 1)
         gram(0, 1, 2)
         interleave("q", 0, 1, "scalar")
@@ -276,10 +265,10 @@ def tile_diffirpriorchannelattention_kernel(tc, q, k, v_bytes, v_scale, temp, u,
         keep_turn("v", 0, 0)
         scale_v(1, 0)
         scale_v(1, 1)
-        quantize("q", 0, 1)
+        quantize("q", 0, 1, 2)
         gram(0, 2, 3)
-        interleave("k", 1, 0, "gpsimd")
         interleave("k", 1, 1, "gpsimd")
+        interleave("k", 1, 0, "gpsimd")
         interleave("q", 1, 0, "gpsimd")
         row_max(0, 0)
         gram(0, 3, 1)
@@ -306,69 +295,67 @@ def tile_diffirpriorchannelattention_kernel(tc, q, k, v_bytes, v_scale, temp, u,
         keep_turn("v", 0, 1)
         keep_turn("pu", 0, 1)
         keep_turn("v", 1, 0)
-        quantize("k", 1, 0)
-        quantize("k", 1, 1)
-        quantize("q", 1, 0)
+        quantize("k", 1, 0, 2)
+        quantize("q", 1, 0, 2)
         gram(1, 0, 6)
         gram(1, 1, 7)
-        quantize("v", 0, 0)
-        quantize("pu", 0, 0)
-        quantize("q", 1, 1)
         gram(1, 2, 1)
-        quantize("v", 0, 1)
-        quantize("pu", 0, 1)
+        quantize("v", 0, 0, 2)
+        quantize("pu", 0, 0, 2)
         mix(0, 0, 2)
-        mix(0, 1, 3)
-        scale_v(1, 2)
-        scale_v(1, 3)
-        square(0, 0)
         row_max(1, 0)
         gram(1, 3, 6)
+        mix(0, 1, 3)
         mix(0, 2, 4)
         mix(0, 3, 5)
         exponential(1, 0)
         row_max(1, 1)
-        turn("v", v_wide, 1, 1, 7)
         exponential(1, 1)
         row_max(1, 2)
         exponential(1, 2)
         invert_sum(1, 0, 1)
         row_max(1, 3)
         exponential(1, 3)
-        square(0, 1)
-        power(0, 0, 2)
+        square(0, 0)
+        root(0, 0, 1)
         invert_sum(1, 1, 2)
         weigh(1, 0)
         invert_sum(1, 2, 3)
         weigh(1, 1)
         turn("pu", pu, 1, 0, 6)
-        square(0, 2)
-        power(0, 2, 3)
-        square(0, 3)
-        keep_turn("pu", 1, 0)
-        keep_turn("v", 1, 1)
         invert_sum(1, 3, 4)
         weigh(1, 2)
         weigh(1, 3)
         turn("pu", pu, 1, 1, 1)
+        scale_v(1, 2)
+        scale_v(1, 3)
+        turn("v", v_wide, 1, 1, 7)
+        keep_turn("pu", 1, 0)
         keep_turn("pu", 1, 1)
-        root(0, 3, 4)
-        quantize("v", 1, 0)
-        quantize("pu", 1, 0)
+        square(0, 1)
+        keep_turn("v", 1, 1)
+        root(0, 1, 2)
+        square(0, 2)
+        square(0, 3)
+        root(0, 2, 4)
+        quantize("v", 1, 0, 1)
+        invert_rms(0, 0, 1)
+        quantize("pu", 1, 0, 1)
         normalize(0, 0)
         spread_shift(0, 2)
-        quantize("v", 1, 1)
-        quantize("pu", 1, 1)
-        mix(1, 0, 7)
+        quantize("pu", 1, 1, 2)
+        mix(1, 0, 6)
         mix(1, 1, 0)
-        mix(1, 2, 6)
+        finish(0, 0, None)
+        invert_rms(0, 1, 2)
+        quantize("v", 1, 1, 2)
+        mix(1, 2, 7)
         mix(1, 3, 1)
         normalize(0, 1)
         finish(0, 1, True)
         spread_shift(1, 3)
+        invert_rms(0, 2, 4)
         normalize(0, 2)
-        invert_rms(0, 3, 4)
-        finish(0, 0, False)
         finish(0, 2, True)
         normalize(0, 3)
         square(1, 0)

@@ -37,39 +37,36 @@ def tile_diffirpriorchannelattention_kernel(tc, q, k, v_bytes, v_scale, temp, u,
         def per_sample(stem, shape, dtype):
             return [sb.tile(shape, dtype, name="%s%d" % (stem, b), align_bytes=64) for b in range(B)]
 
-        def per_part(stem, parts, shape, dtype):
+        def per_tile(stem, dtype):
             return [
-                [sb.tile(shape, dtype, name="%s%d_%d" % (stem, b, t), align_bytes=64) for t in range(parts)]
+                [sb.tile([P, C], dtype, name="%s%d_%d" % (stem, b, t), align_bytes=64) for t in range(TILES)]
                 for b in range(B)
             ]
 
-        q_raw = per_sample("q_raw", [P, PACK, C], BF16)
-        k_raw = per_sample("k_raw", [P, PACK, C], BF16)
+        operands = ("q", "k", "v", "pu")
+        tokens = {"q": per_sample("q_tokens", [P, PACK, C], BF16), "k": per_sample("k_tokens", [P, PACK, C], BF16)}
         v_raw = per_sample("v_raw", [P, TILES, C], U8)
-        staged = [sb.tile([P, C * PACK], BF16, name="staged%d" % s, align_bytes=64) for s in range(2)]
-        k_grouped = [staged[0], staged[1]]
-        q_grouped = [staged[1], staged[0]]
-        v_grouped = per_sample("v_grouped", [P, C * PACK], BF16)
-        pu_grouped = per_sample("pu_grouped", [P, C * PACK], BF16)
-        codes = {name: per_sample(name + "_codes", [P, C], U32) for name in ("q", "k", "v", "pu")}
-        scales = {name: per_sample(name + "_scales", [P, C], U8) for name in ("q", "k", "v", "pu")}
-        grouped = {"q": q_grouped, "k": k_grouped, "v": v_grouped, "pu": pu_grouped}
-        raw = {"q": q_raw, "k": k_raw}
-        v_wide = per_part("v_wide", TILES, [P, C], BF16)
-        neg_a = per_part("neg_a", TILES, [P, C], F32)
-        e = per_part("e", TILES, [P, C], F32)
-        pu = per_part("pu", TILES, [P, C], BF16)
-        gained = per_part("gained", TILES, [P, C], F32)
-        result = per_part("result", TILES, [P, C], F32)
+        first_k, first_q = per_sample("qk_grouped", [P, C * PACK], BF16)
+        grouped = {
+            "q": [first_q, first_k],
+            "k": [first_k, first_q],
+            "v": per_sample("v_grouped", [P, C * PACK], BF16),
+            "pu": per_sample("pu_grouped", [P, C * PACK], BF16),
+        }
+        codes = {name: per_sample(name + "_codes", [P, C], U32) for name in operands}
+        scales = {name: per_sample(name + "_scales", [P, C], U8) for name in operands}
+        rounded = {"v": per_tile("v_rounded", BF16), "pu": per_tile("pu_rounded", BF16)}
+        neg_a = per_tile("neg_a", F32)
+        e = per_tile("e", F32)
+        gained = per_tile("gained", F32)
+        result = per_tile("result", F32)
         neg_max = per_sample("neg_max", [P, TILES], F32)
         e_sum = per_sample("e_sum", [P, TILES], F32)
         inv_sum = per_sample("inv_sum", [P, TILES], F32)
         mean_sq = per_sample("mean_sq", [P, TILES], F32)
-        rms = per_sample("rms", [P, TILES], F32)
         inv_rms = per_sample("inv_rms", [P, TILES], F32)
         gain = per_sample("gain", [P, C], F32)
-        shift = sb.tile([P, B, C], BF16, name="shift")
-        squares = sb.tile([P, C], BF16, name="squares")
+        shift0 = sb.tile([P, C], BF16, name="shift0")
         rows = sb.tile([P, P], BF16, name="rows")
         ident32 = sb.tile([P, P], F32, name="ident32")
         ident16 = sb.tile([P, P], BF16, name="ident16")
@@ -78,76 +75,77 @@ def tile_diffirpriorchannelattention_kernel(tc, q, k, v_bytes, v_scale, temp, u,
         neg_temp = sb.tile([P, TILES], F32, name="neg_temp")
         u_cols = sb.tile([P, TILES], F32, name="u_cols")
         gain_cols = sb.tile([P, B * TILES], F32, name="gain_cols")
+        shift1_cols = sb.tile([P, TILES], F32, name="shift1_cols")
 
-        shift_cols = sb.tile([P, B * TILES], F32, name="shift_cols")
-        warm = sb.tile([P, 2], F32, name="warm")
+        temp_rows = slice(0, TILES)
+        u_rows = slice(TILES, 2 * TILES)
+        zs_rows = slice(2 * TILES, (2 + B) * TILES)
+        zb1_rows = slice((2 + B) * TILES, (3 + B) * TILES)
         nc.vector.memset(rows[:], 0.0)
-        nc.vector.memset(warm[:, 0:1], 0.0)
         make_identity(nc, ident32[:])
         nc.vector.tensor_copy(out=ident16[:], in_=ident32[:])
 
         def load_tokens(name, source, b):
-            nc.sync.dma_start(out=raw[name][b][:], in_=source[b].rearrange("(p j) c -> p j c", j=PACK))
+            nc.sync.dma_start(out=tokens[name][b][:], in_=source[b].rearrange("(p j) c -> p j c", j=PACK))
 
         def load_v(b):
-            nc.sync.dma_start(out=v_raw[b][:], in_=v_bytes[b].rearrange("(p m) c -> p m c", m=TILES))
+            nc.sync.dma_start(out=v_raw[b][:], in_=v_bytes[b].rearrange("(p t) c -> p t c", t=TILES))
 
-        nc.sync.dma_start(out=vs_cols[:], in_=v_scale.rearrange("a b (p t) -> p (a b t)", t=PACK))
-        nc.scalar.dma_start(out=rows[0:4, :], in_=temp.rearrange("(t p) -> t p", p=P))
-        nc.scalar.dma_start(out=rows[4:8, :], in_=u.rearrange("(t p) -> t p", p=P))
-        nc.scalar.dma_start(out=rows[8:16, :], in_=zs.rearrange("b (t p) -> (b t) p", p=P))
-        nc.scalar.dma_start(out=rows[16:24, :], in_=zb.rearrange("b (t p) -> (b t) p", p=P))
-        nc.scalar.activation(out=warm[:, 1:2], in_=warm[:, 0:1], func=ACT.Exp)
+        nc.sync.dma_start(out=vs_cols[:], in_=v_scale.rearrange("a b (p j) -> p (a b j)", j=PACK))
+        nc.scalar.dma_start(out=rows[temp_rows, :], in_=temp.rearrange("(t p) -> t p", p=P))
+        nc.scalar.dma_start(out=rows[u_rows, :], in_=u.rearrange("(t p) -> t p", p=P))
+        nc.scalar.dma_start(out=rows[zs_rows, :], in_=zs.rearrange("b (t p) -> (b t) p", p=P))
+        nc.scalar.dma_start(out=rows[zb1_rows, :], in_=zb[1].rearrange("(t p) -> t p", p=P))
         load_tokens("k", k, 0)
         load_v(0)
         load_tokens("q", q, 0)
         load_v(1)
         load_tokens("k", k, 1)
         load_tokens("q", q, 1)
-        nc.sync.dma_start(
-            out=shift[:].rearrange("p b c -> p (b c)"),
-            in_=zb.rearrange("b c -> (b c)").partition_broadcast(P),
-        )
+        nc.sync.dma_start(out=shift0[:], in_=zb[0].partition_broadcast(P))
 
         vs_bank = bank(2, [P, C], F32, "vs_bank")
-        for t in range(PACK):
-            nc.tensor.transpose(vs_bank[:, t::PACK], vs_cols[:, t : t + 1].to_broadcast([P, P]), ident32[:])
-        nc.scalar.copy(out=vs_all[:], in_=vs_bank[:])
+        for j in range(PACK):
+            nc.tensor.transpose(vs_bank[:, j::PACK], vs_cols[:, j : j + 1].to_broadcast([P, P]), ident32[:])
+        nc.scalar.activation(out=vs_all[:], in_=vs_bank[:], func=ACT.Copy)
 
         cols_bank = bank(1, [P, P], BF16, "cols_bank")
         nc.tensor.transpose(cols_bank[:], rows[:], ident16[:])
-        nc.scalar.activation(out=u_cols[:], in_=cols_bank[:, 4:8], func=ACT.Copy, scale=math.sqrt(C))
-        nc.scalar.activation(out=gain_cols[:], in_=cols_bank[:, 8:16], func=ACT.Copy, bias=1.0)
-        nc.scalar.activation(out=neg_temp[:], in_=cols_bank[:, 0:4], func=ACT.Copy, scale=-1.0 / math.sqrt(N))
+        nc.scalar.activation(out=u_cols[:], in_=cols_bank[:, u_rows], func=ACT.Copy, scale=math.sqrt(C))
+        nc.scalar.activation(out=gain_cols[:], in_=cols_bank[:, zs_rows], func=ACT.Copy, bias=1.0)
+        nc.scalar.activation(out=neg_temp[:], in_=cols_bank[:, temp_rows], func=ACT.Copy, scale=-1.0 / math.sqrt(N))
+        nc.scalar.activation(out=shift1_cols[:], in_=cols_bank[:, zb1_rows], func=ACT.Copy)
 
-        nc.scalar.activation(out=shift_cols[:], in_=cols_bank[:, 16:24], func=ACT.Copy)
-
-        def spread(target, cols, first):
+        def spread(number, cols, name):
+            target = bank(number, [P, C], F32, name)
             for t in range(TILES):
-                column = cols[:, first + t : first + t + 1]
-                nc.tensor.transpose(target[:, t * P : (t + 1) * P], column.to_broadcast([P, P]), ident32[:])
+                nc.tensor.transpose(target[:, t * P : (t + 1) * P], cols[:, t : t + 1].to_broadcast([P, P]), ident32[:])
+            return target
 
-        gain_banks = [bank(6 + b, [P, C], F32, "gain_bank%d" % b) for b in range(B)]
-        for b in range(B):
-            spread(gain_banks[b], gain_cols, b * TILES)
-        u_bank = bank(0, [P, C], F32, "u_bank")
-        spread(u_bank, u_cols, 0)
+        gain_banks, gram_banks, turned_banks, o_banks = {}, {}, {}, {}
 
-        gram_banks, o_banks, turn_banks, shift_banks = {}, {}, {}, {}
+        def half_of(name, b, h):
+            return grouped[name][b][:, h * HALF * PACK : (h + 1) * HALF * PACK]
+
+        def spread_gain(b, number):
+            gain_banks[b] = spread(number, gain_cols[:, b * TILES : (b + 1) * TILES], "gain_bank%d" % b)
 
         def keep_gain(b):
             nc.scalar.copy(out=gain[b][:], in_=gain_banks[b][:])
 
-        def interleave(name, b, h, engine):
-            source = raw[name][b][:, :, h * HALF : (h + 1) * HALF].rearrange("p j (c i) -> p c j i", i=RUN)
-            target = grouped[name][b][:, h * HALF * PACK : (h + 1) * HALF * PACK]
-            target = target.rearrange("p (c i j) -> p c j i", i=RUN, j=PACK)
-            if engine == "vector":
-                nc.vector.tensor_copy(out=target, in_=source)
-            elif engine == "scalar":
-                nc.scalar.copy(out=target, in_=source)
-            else:
-                nc.gpsimd.tensor_scalar(out=target, in0=source, scalar1=1.0, scalar2=0.0, op0=ALU.mult, op1=ALU.add)
+        def interleave(copy, name, b, h):
+            source = tokens[name][b][:, :, h * HALF : (h + 1) * HALF]
+            copy(
+                out=half_of(name, b, h).rearrange("p (c i j) -> p c j i", i=RUN, j=PACK),
+                in_=source.rearrange("p j (c i) -> p c j i", i=RUN),
+            )
+
+        def interleave_on_gpsimd(name, b, h):
+            source = tokens[name][b][:, :, h * HALF : (h + 1) * HALF]
+            nc.gpsimd.tensor_scalar(
+                out=half_of(name, b, h).rearrange("p (c j) -> p c j", j=PACK), in0=source.rearrange("p j c -> p c j"),
+                scalar1=1.0, scalar2=0.0, op0=ALU.mult, op1=ALU.add,
+            )
 
         def quantize(name, b, first, last):
             cols = slice(first * HALF, last * HALF)
@@ -157,7 +155,8 @@ def tile_diffirpriorchannelattention_kernel(tc, q, k, v_bytes, v_scale, temp, u,
                 in_=grouped[name][b][:, first * HALF * PACK : last * HALF * PACK],
             )
 
-        def product(target, left, right, b, t):
+        def product(left, right, b, t, number):
+            target = bank(number, [P, C], F32, "%s_%s%d_%d" % (left, right, b, t))
             cols = slice(t * P, (t + 1) * P)
             nc.tensor.matmul_mx(
                 out=target[:],
@@ -168,10 +167,10 @@ def tile_diffirpriorchannelattention_kernel(tc, q, k, v_bytes, v_scale, temp, u,
                 start=True,
                 stop=True,
             )
+            return target
 
         def gram(b, t, number):
-            gram_banks[b, t] = bank(number, [P, C], F32, "gram%d_%d" % (b, t))
-            product(gram_banks[b, t], "q", "k", b, t)
+            gram_banks[b, t] = product("q", "k", b, t, number)
 
         def row_max(b, t):
             nc.vector.tensor_scalar(
@@ -185,47 +184,46 @@ def tile_diffirpriorchannelattention_kernel(tc, q, k, v_bytes, v_scale, temp, u,
                 bias=neg_max[b][:, t : t + 1], accum_out=e_sum[b][:, t : t + 1],
             )
 
-        def invert_sum(b, first, last):
-            nc.vector.reciprocal(out=inv_sum[b][:, first:last], in_=e_sum[b][:, first:last])
+        def invert_sum(b, t):
+            nc.vector.reciprocal(out=inv_sum[b][:, t : t + 1], in_=e_sum[b][:, t : t + 1])
 
         def weigh(b, t):
             nc.vector.scalar_tensor_tensor(
-                out=pu[b][t][:], in0=e[b][t][:], scalar=inv_sum[b][:, t : t + 1], in1=u_bank[:],
+                out=rounded["pu"][b][t][:], in0=e[b][t][:], scalar=inv_sum[b][:, t : t + 1], in1=u_bank[:],
                 op0=ALU.mult, op1=ALU.mult,
             )
 
         def scale_v(b, t):
-            nc.vector.tensor_tensor(out=v_wide[b][t][:], in0=v_raw[b][:, t, :].bitcast(FP8), in1=vs_all[:], op=ALU.mult)
+            nc.vector.tensor_tensor(
+                out=rounded["v"][b][t][:], in0=v_raw[b][:, t, :].bitcast(FP8), in1=vs_all[:], op=ALU.mult
+            )
 
-        def turn(name, source, b, h, number):
-            turn_banks[name, b, h] = bank(number, [P, 2, 2, P], F32, "turn_%s%d_%d" % (name, b, h))
+        def turn(name, b, h, number):
+            turned_banks[name, b, h] = bank(number, [P, 2, 2, P], F32, "turned_%s%d_%d" % (name, b, h))
             for s in range(2):
-                words = source[b][2 * h + s][:].bitcast(F32)
+                words = rounded[name][b][2 * h + s][:].bitcast(F32)
                 for w in range(2):
-                    nc.tensor.transpose(turn_banks[name, b, h][:, s, w, :], words[:, w::2], ident32[:])
+                    nc.tensor.transpose(turned_banks[name, b, h][:, s, w, :], words[:, w::2], ident32[:])
 
-        def keep_turn(name, b, h):
-            target = grouped[name][b][:, h * HALF * PACK : (h + 1) * HALF * PACK].bitcast(F32)
+        def keep_turned(name, b, h):
             nc.scalar.copy(
-                out=target.rearrange("p (s r w) -> p s r w", s=2, w=2),
-                in_=turn_banks[name, b, h][:].rearrange("p s w r -> p s r w"),
+                out=half_of(name, b, h).bitcast(F32).rearrange("p (s r w) -> p s r w", s=2, w=2),
+                in_=turned_banks[name, b, h][:].rearrange("p s w r -> p s r w"),
             )
 
         def mix(b, t, number):
-            o_banks[b, t] = bank(number, [P, C], F32, "o%d_%d" % (b, t))
-            product(o_banks[b, t], "v", "pu", b, t)
+            o_banks[b, t] = product("v", "pu", b, t, number)
 
         def square(b, t):
             nc.scalar.activation(
-                out=squares[:], in_=o_banks[b, t][:], func=ACT.Square, scale=1.0 / math.sqrt(C),
+                out=neg_a[b][t][:], in_=o_banks[b, t][:], func=ACT.Square, scale=1.0 / math.sqrt(C),
                 accum_out=mean_sq[b][:, t : t + 1],
             )
 
-        def root(b, first, last):
-            nc.scalar.activation(out=rms[b][:, first:last], in_=mean_sq[b][:, first:last], func=ACT.Sqrt, bias=EPS)
-
-        def invert_rms(b, first, last):
-            nc.vector.reciprocal(out=inv_rms[b][:, first:last], in_=rms[b][:, first:last])
+        def inverse_root(b, t):
+            nc.scalar.activation(
+                out=inv_rms[b][:, t : t + 1], in_=mean_sq[b][:, t : t + 1], func=ACT.Abs_reciprocal_sqrt, bias=EPS
+            )
 
         def normalize(b, t):
             nc.vector.scalar_tensor_tensor(
@@ -233,148 +231,115 @@ def tile_diffirpriorchannelattention_kernel(tc, q, k, v_bytes, v_scale, temp, u,
                 op0=ALU.mult, op1=ALU.mult,
             )
 
-        def spread_shift(b, number):
-            shift_banks[b] = bank(number, [P, C], F32, "shift_bank%d" % b)
-            spread(shift_banks[b], shift_cols, b * TILES)
+        def finish(engine, b, t, shift):
+            engine.tensor_tensor(out=result[b][t][:], in0=gained[b][t][:], in1=shift[:], op=ALU.add)
+            nc.sync.dma_start(out=out[b].rearrange("(p t) c -> p t c", t=TILES)[:, t, :], in_=result[b][t][:])
 
-        def finish(b, t, on_gpsimd):
-            if on_gpsimd is None:
-                nc.vector.tensor_tensor(out=result[b][t][:], in0=gained[b][t][:], in1=shift[:, b, :], op=ALU.add)
-            elif on_gpsimd:
-                nc.gpsimd.tensor_tensor(out=result[b][t][:], in0=gained[b][t][:], in1=shift[:, b, :], op=ALU.add)
-            else:
-                nc.vector.tensor_tensor(out=result[b][t][:], in0=gained[b][t][:], in1=shift_banks[b][:], op=ALU.add)
-            nc.sync.dma_start(out=out[b].rearrange("(p m) c -> p m c", m=TILES)[:, t, :], in_=result[b][t][:])
+        def rest_of_softmax(b, numbers):
+            exponential(b, 0)
+            for t in range(1, TILES):
+                if t == TILES - 1:
+                    invert_sum(b, 0)
+                row_max(b, t)
+                exponential(b, t)
+            for t in range(TILES):
+                if t + 1 < TILES:
+                    invert_sum(b, t + 1)
+                weigh(b, t)
+                if t % 2 == 1:
+                    turn("pu", b, t // 2, numbers[t // 2])
 
-        interleave("k", 0, 0, "vector")
-        interleave("k", 0, 1, "scalar")
+        u_bank = spread(0, u_cols, "u_bank")
+
+        spread_gain(0, 6)
+        interleave(nc.vector.tensor_copy, "k", 0, 0)
+        interleave(nc.scalar.copy, "k", 0, 1)
         scale_v(0, 0)
         scale_v(0, 1)
-        turn("v", v_wide, 0, 0, 4)
-        interleave("q", 0, 0, "scalar")
+        turn("v", 0, 0, 4)
+        spread_gain(1, 7)
+        interleave(nc.scalar.copy, "q", 0, 0)
         scale_v(0, 2)
-        quantize("k", 0, 0, 2)
         scale_v(0, 3)
-        turn("v", v_wide, 0, 1, 5)
+        quantize("k", 0, 0, 2)
         quantize("q", 0, 0, 1)
         gram(0, 0, 1)
         gram(0, 1, 2)
-        interleave("q", 0, 1, "scalar")
-        keep_gain(0)
-        keep_gain(1)
-        keep_turn("v", 0, 0)
+        interleave(nc.scalar.copy, "q", 0, 1)
+        keep_turned("v", 0, 0)
+        interleave(nc.scalar.copy, "q", 1, 1)
         scale_v(1, 0)
         scale_v(1, 1)
         quantize("q", 0, 1, 2)
         gram(0, 2, 3)
-        interleave("k", 1, 1, "gpsimd")
-        interleave("k", 1, 0, "gpsimd")
-        interleave("q", 1, 0, "gpsimd")
+
+        interleave_on_gpsimd("k", 1, 1)
+        interleave_on_gpsimd("k", 1, 0)
         row_max(0, 0)
         gram(0, 3, 1)
-        turn("v", v_wide, 1, 0, 4)
-        exponential(0, 0)
-        row_max(0, 1)
-        exponential(0, 1)
-        row_max(0, 2)
-        exponential(0, 2)
-        invert_sum(0, 0, 1)
-        row_max(0, 3)
-        exponential(0, 3)
-        invert_sum(0, 1, 2)
-        weigh(0, 0)
-        invert_sum(0, 2, 3)
-        weigh(0, 1)
-        turn("pu", pu, 0, 0, 2)
-        invert_sum(0, 3, 4)
-        weigh(0, 2)
-        weigh(0, 3)
-        turn("pu", pu, 0, 1, 3)
-        interleave("q", 1, 1, "scalar")
-        keep_turn("pu", 0, 0)
-        keep_turn("v", 0, 1)
-        keep_turn("pu", 0, 1)
-        keep_turn("v", 1, 0)
+        turn("v", 0, 1, 5)
+        turn("v", 1, 0, 4)
+        rest_of_softmax(0, (2, 3))
+
+        interleave(nc.scalar.copy, "q", 1, 0)
+        keep_turned("v", 0, 1)
+        for h in range(2):
+            keep_turned("pu", 0, h)
+        for b in range(B):
+            keep_gain(b)
+        keep_turned("v", 1, 0)
         quantize("k", 1, 0, 2)
         quantize("q", 1, 0, 2)
-        gram(1, 0, 6)
-        gram(1, 1, 7)
-        gram(1, 2, 1)
+        gram(1, 0, 1)
+        gram(1, 1, 5)
         quantize("v", 0, 0, 2)
         quantize("pu", 0, 0, 2)
-        mix(0, 0, 2)
+
         row_max(1, 0)
-        gram(1, 3, 6)
-        mix(0, 1, 3)
-        mix(0, 2, 4)
-        mix(0, 3, 5)
-        exponential(1, 0)
-        row_max(1, 1)
-        exponential(1, 1)
-        row_max(1, 2)
-        exponential(1, 2)
-        invert_sum(1, 0, 1)
-        row_max(1, 3)
-        exponential(1, 3)
+        gram(1, 2, 6)
+        gram(1, 3, 1)
+        for t, number in enumerate((2, 3, 4, 7)):
+            mix(0, t, number)
+        rest_of_softmax(1, (5, 1))
+
         square(0, 0)
-        root(0, 0, 1)
-        invert_sum(1, 1, 2)
-        weigh(1, 0)
-        invert_sum(1, 2, 3)
-        weigh(1, 1)
-        turn("pu", pu, 1, 0, 6)
-        invert_sum(1, 3, 4)
-        weigh(1, 2)
-        weigh(1, 3)
-        turn("pu", pu, 1, 1, 1)
+        inverse_root(0, 0)
         scale_v(1, 2)
         scale_v(1, 3)
-        turn("v", v_wide, 1, 1, 7)
-        keep_turn("pu", 1, 0)
-        keep_turn("pu", 1, 1)
+        turn("v", 1, 1, 6)
+        for h in range(2):
+            keep_turned("pu", 1, h)
         square(0, 1)
-        keep_turn("v", 1, 1)
-        root(0, 1, 2)
-        square(0, 2)
-        square(0, 3)
-        root(0, 2, 4)
+        keep_turned("v", 1, 1)
+        inverse_root(0, 1)
         quantize("v", 1, 0, 1)
-        invert_rms(0, 0, 1)
         quantize("pu", 1, 0, 1)
         normalize(0, 0)
-        spread_shift(0, 2)
+        shift1_bank = spread(2, shift1_cols, "shift1_bank")
         quantize("pu", 1, 1, 2)
-        mix(1, 0, 6)
+        mix(1, 0, 5)
         mix(1, 1, 0)
-        finish(0, 0, None)
-        invert_rms(0, 1, 2)
+        finish(nc.vector, 0, 0, shift0)
         quantize("v", 1, 1, 2)
-        mix(1, 2, 7)
+        mix(1, 2, 6)
         mix(1, 3, 1)
-        normalize(0, 1)
-        finish(0, 1, True)
-        spread_shift(1, 3)
-        invert_rms(0, 2, 4)
-        normalize(0, 2)
-        finish(0, 2, True)
+
+        remaining = [(0, 2), (0, 3)] + [(1, t) for t in range(TILES)]
+        square(*remaining[0])
+        for done, following in zip(remaining, remaining[1:]):
+            square(*following)
+            inverse_root(*done)
+        inverse_root(*remaining[-1])
+
+        for t in (1, 2):
+            normalize(0, t)
+            finish(nc.gpsimd, 0, t, shift0)
         normalize(0, 3)
-        square(1, 0)
-        square(1, 1)
-        root(1, 0, 1)
-        square(1, 2)
-        root(1, 1, 2)
-        square(1, 3)
-        root(1, 2, 3)
-        root(1, 3, 4)
-        invert_rms(1, 0, 1)
-        finish(0, 3, False)
-        invert_rms(1, 1, 2)
         normalize(1, 0)
-        finish(1, 0, True)
         normalize(1, 1)
-        invert_rms(1, 2, 4)
-        finish(1, 1, False)
-        normalize(1, 2)
-        normalize(1, 3)
-        finish(1, 2, False)
-        finish(1, 3, False)
+        finish(nc.vector, 1, 0, shift1_bank)
+        finish(nc.gpsimd, 0, 3, shift0)
+        for t in (2, 3):
+            normalize(1, t)
+            finish(nc.vector, 1, t - 1, shift1_bank)
+        finish(nc.vector, 1, 3, shift1_bank)

import math
from contextlib import ExitStack

import concourse.mybir as mybir
from concourse.masks import make_identity

B, N, C = 2, 512, 512
EPS = 1e-6
FLOPS = 2 * B * (N * C * C + N * C * C)

F32 = mybir.dt.float32
BF16 = mybir.dt.bfloat16
U32 = mybir.dt.uint32
U8 = mybir.dt.uint8
FP8 = mybir.dt.float8_e4m3fn
FP8X4 = mybir.dt.float8_e4m3fn_x4
ALU = mybir.AluOpType
ACT = mybir.ActivationFunctionType

P = 128
PACK = 4
TILES = 4
HALF = C // 2
RUN = 4


def tile_diffirpriorchannelattention_kernel(tc, q, k, v_bytes, v_scale, temp, u, zs, zb, out):
    nc = tc.nc
    with ExitStack() as ctx:
        sb = ctx.enter_context(tc.tile_pool(name="sb", bufs=1))
        psum = ctx.enter_context(tc.psum_pool(name="psum", bufs=1))
        ctx.enter_context(tc.manual_schedule())

        def bank(number, shape, dtype, name):
            return psum.tile(shape, dtype, name=name, tag="bank%d" % number)

        def per_sample(stem, shape, dtype):
            return [sb.tile(shape, dtype, name="%s%d" % (stem, b), align_bytes=64) for b in range(B)]

        def per_tile(stem, dtype):
            return [
                [sb.tile([P, C], dtype, name="%s%d_%d" % (stem, b, t), align_bytes=64) for t in range(TILES)]
                for b in range(B)
            ]

        operands = ("q", "k", "v", "pu")
        tokens = {"q": per_sample("q_tokens", [P, PACK, C], BF16), "k": per_sample("k_tokens", [P, PACK, C], BF16)}
        v_raw = per_sample("v_raw", [P, TILES, C], U8)
        first_k, first_q = per_sample("qk_grouped", [P, C * PACK], BF16)
        grouped = {
            "q": [first_q, first_k],
            "k": [first_k, first_q],
            "v": per_sample("v_grouped", [P, C * PACK], BF16),
            "pu": per_sample("pu_grouped", [P, C * PACK], BF16),
        }
        codes = {name: per_sample(name + "_codes", [P, C], U32) for name in operands}
        scales = {name: per_sample(name + "_scales", [P, C], U8) for name in operands}
        rounded = {"v": per_tile("v_rounded", BF16), "pu": per_tile("pu_rounded", BF16)}
        neg_a = per_tile("neg_a", F32)
        e = per_tile("e", F32)
        gained = per_tile("gained", F32)
        result = per_tile("result", F32)
        neg_max = per_sample("neg_max", [P, TILES], F32)
        e_sum = per_sample("e_sum", [P, TILES], F32)
        inv_sum = per_sample("inv_sum", [P, TILES], F32)
        mean_sq = per_sample("mean_sq", [P, TILES], F32)
        inv_rms = per_sample("inv_rms", [P, TILES], F32)
        gain = per_sample("gain", [P, C], F32)
        shift0 = sb.tile([P, C], BF16, name="shift0")
        rows = sb.tile([P, P], BF16, name="rows")
        ident32 = sb.tile([P, P], F32, name="ident32")
        ident16 = sb.tile([P, P], BF16, name="ident16")
        vs_cols = sb.tile([P, PACK], F32, name="vs_cols")
        vs_all = sb.tile([P, C], F32, name="vs_all")
        neg_temp = sb.tile([P, TILES], F32, name="neg_temp")
        u_cols = sb.tile([P, TILES], F32, name="u_cols")
        gain_cols = sb.tile([P, B * TILES], F32, name="gain_cols")
        shift1_cols = sb.tile([P, TILES], F32, name="shift1_cols")

        temp_rows = slice(0, TILES)
        u_rows = slice(TILES, 2 * TILES)
        zs_rows = slice(2 * TILES, (2 + B) * TILES)
        zb1_rows = slice((2 + B) * TILES, (3 + B) * TILES)
        nc.vector.memset(rows[:], 0.0)
        make_identity(nc, ident32[:])
        nc.vector.tensor_copy(out=ident16[:], in_=ident32[:])

        def load_tokens(name, source, b):
            nc.sync.dma_start(out=tokens[name][b][:], in_=source[b].rearrange("(p j) c -> p j c", j=PACK))

        def load_v(b):
            nc.sync.dma_start(out=v_raw[b][:], in_=v_bytes[b].rearrange("(p t) c -> p t c", t=TILES))

        nc.sync.dma_start(out=vs_cols[:], in_=v_scale.rearrange("a b (p j) -> p (a b j)", j=PACK))
        nc.scalar.dma_start(out=rows[temp_rows, :], in_=temp.rearrange("(t p) -> t p", p=P))
        nc.scalar.dma_start(out=rows[u_rows, :], in_=u.rearrange("(t p) -> t p", p=P))
        nc.scalar.dma_start(out=rows[zs_rows, :], in_=zs.rearrange("b (t p) -> (b t) p", p=P))
        nc.scalar.dma_start(out=rows[zb1_rows, :], in_=zb[1].rearrange("(t p) -> t p", p=P))
        load_tokens("k", k, 0)
        load_v(0)
        load_tokens("q", q, 0)
        load_v(1)
        load_tokens("k", k, 1)
        load_tokens("q", q, 1)
        nc.sync.dma_start(out=shift0[:], in_=zb[0].partition_broadcast(P))

        vs_bank = bank(2, [P, C], F32, "vs_bank")
        for j in range(PACK):
            nc.tensor.transpose(vs_bank[:, j::PACK], vs_cols[:, j : j + 1].to_broadcast([P, P]), ident32[:])
        nc.scalar.activation(out=vs_all[:], in_=vs_bank[:], func=ACT.Copy)

        cols_bank = bank(1, [P, P], BF16, "cols_bank")
        nc.tensor.transpose(cols_bank[:], rows[:], ident16[:])
        nc.scalar.activation(out=u_cols[:], in_=cols_bank[:, u_rows], func=ACT.Copy, scale=math.sqrt(C))
        nc.scalar.activation(out=gain_cols[:], in_=cols_bank[:, zs_rows], func=ACT.Copy, bias=1.0)
        nc.scalar.activation(out=neg_temp[:], in_=cols_bank[:, temp_rows], func=ACT.Copy, scale=-1.0 / math.sqrt(N))
        nc.scalar.activation(out=shift1_cols[:], in_=cols_bank[:, zb1_rows], func=ACT.Copy)

        def spread(number, cols, name):
            target = bank(number, [P, C], F32, name)
            for t in range(TILES):
                nc.tensor.transpose(target[:, t * P : (t + 1) * P], cols[:, t : t + 1].to_broadcast([P, P]), ident32[:])
            return target

        gain_banks, gram_banks, turned_banks, o_banks = {}, {}, {}, {}

        def half_of(name, b, h):
            return grouped[name][b][:, h * HALF * PACK : (h + 1) * HALF * PACK]

        def spread_gain(b, number):
            gain_banks[b] = spread(number, gain_cols[:, b * TILES : (b + 1) * TILES], "gain_bank%d" % b)

        def keep_gain(b):
            nc.scalar.copy(out=gain[b][:], in_=gain_banks[b][:])

        def interleave(copy, name, b, h):
            source = tokens[name][b][:, :, h * HALF : (h + 1) * HALF]
            copy(
                out=half_of(name, b, h).rearrange("p (c i j) -> p c j i", i=RUN, j=PACK),
                in_=source.rearrange("p j (c i) -> p c j i", i=RUN),
            )

        def interleave_on_gpsimd(name, b, h):
            source = tokens[name][b][:, :, h * HALF : (h + 1) * HALF]
            nc.gpsimd.tensor_scalar(
                out=half_of(name, b, h).rearrange("p (c j) -> p c j", j=PACK), in0=source.rearrange("p j c -> p c j"),
                scalar1=1.0, scalar2=0.0, op0=ALU.mult, op1=ALU.add,
            )

        def quantize(name, b, first, last):
            cols = slice(first * HALF, last * HALF)
            nc.vector.quantize_mx(
                out=codes[name][b][:, cols].bitcast(FP8X4),
                scales=scales[name][b][:, cols],
                in_=grouped[name][b][:, first * HALF * PACK : last * HALF * PACK],
            )

        def product(left, right, b, t, number):
            target = bank(number, [P, C], F32, "%s_%s%d_%d" % (left, right, b, t))
            cols = slice(t * P, (t + 1) * P)
            nc.tensor.matmul_mx(
                out=target[:],
                lhsT=codes[left][b][:, cols].bitcast(FP8X4),
                lhsT_scale=scales[left][b][:, cols],
                rhs=codes[right][b][:].bitcast(FP8X4),
                rhs_scale=scales[right][b][:],
                start=True,
                stop=True,
            )
            return target

        def gram(b, t, number):
            gram_banks[b, t] = product("q", "k", b, t, number)

        def row_max(b, t):
            nc.vector.tensor_scalar(
                out=neg_a[b][t][:], in0=gram_banks[b, t][:], scalar1=neg_temp[:, t : t + 1], scalar2=None,
                op0=ALU.mult, op1=ALU.min, accum_out=neg_max[b][:, t : t + 1],
            )

        def exponential(b, t):
            nc.scalar.activation(
                out=e[b][t][:], in_=neg_a[b][t][:], func=ACT.Exp, scale=-1.0,
                bias=neg_max[b][:, t : t + 1], accum_out=e_sum[b][:, t : t + 1],
            )

        def invert_sum(b, t):
            nc.vector.reciprocal(out=inv_sum[b][:, t : t + 1], in_=e_sum[b][:, t : t + 1])

        def weigh(b, t):
            nc.vector.scalar_tensor_tensor(
                out=rounded["pu"][b][t][:], in0=e[b][t][:], scalar=inv_sum[b][:, t : t + 1], in1=u_bank[:],
                op0=ALU.mult, op1=ALU.mult,
            )

        def scale_v(b, t):
            nc.vector.tensor_tensor(
                out=rounded["v"][b][t][:], in0=v_raw[b][:, t, :].bitcast(FP8), in1=vs_all[:], op=ALU.mult
            )

        def turn(name, b, h, number):
            turned_banks[name, b, h] = bank(number, [P, 2, 2, P], F32, "turned_%s%d_%d" % (name, b, h))
            for s in range(2):
                words = rounded[name][b][2 * h + s][:].bitcast(F32)
                for w in range(2):
                    nc.tensor.transpose(turned_banks[name, b, h][:, s, w, :], words[:, w::2], ident32[:])

        def keep_turned(name, b, h):
            nc.scalar.copy(
                out=half_of(name, b, h).bitcast(F32).rearrange("p (s r w) -> p s r w", s=2, w=2),
                in_=turned_banks[name, b, h][:].rearrange("p s w r -> p s r w"),
            )

        def mix(b, t, number):
            o_banks[b, t] = product("v", "pu", b, t, number)

        def square(b, t):
            nc.scalar.activation(
                out=neg_a[b][t][:], in_=o_banks[b, t][:], func=ACT.Square, scale=1.0 / math.sqrt(C),
                accum_out=mean_sq[b][:, t : t + 1],
            )

        def inverse_root(b, t):
            nc.scalar.activation(
                out=inv_rms[b][:, t : t + 1], in_=mean_sq[b][:, t : t + 1], func=ACT.Abs_reciprocal_sqrt, bias=EPS
            )

        def normalize(b, t):
            nc.vector.scalar_tensor_tensor(
                out=gained[b][t][:], in0=o_banks[b, t][:], scalar=inv_rms[b][:, t : t + 1], in1=gain[b][:],
                op0=ALU.mult, op1=ALU.mult,
            )

        def finish(engine, b, t, shift):
            engine.tensor_tensor(out=result[b][t][:], in0=gained[b][t][:], in1=shift[:], op=ALU.add)
            nc.sync.dma_start(out=out[b].rearrange("(p t) c -> p t c", t=TILES)[:, t, :], in_=result[b][t][:])

        def rest_of_softmax(b, numbers):
            exponential(b, 0)
            for t in range(1, TILES):
                if t == TILES - 1:
                    invert_sum(b, 0)
                row_max(b, t)
                exponential(b, t)
            for t in range(TILES):
                if t + 1 < TILES:
                    invert_sum(b, t + 1)
                weigh(b, t)
                if t % 2 == 1:
                    turn("pu", b, t // 2, numbers[t // 2])

        u_bank = spread(0, u_cols, "u_bank")

        spread_gain(0, 6)
        interleave(nc.vector.tensor_copy, "k", 0, 0)
        interleave(nc.scalar.copy, "k", 0, 1)
        scale_v(0, 0)
        scale_v(0, 1)
        turn("v", 0, 0, 4)
        spread_gain(1, 7)
        interleave(nc.scalar.copy, "q", 0, 0)
        scale_v(0, 2)
        scale_v(0, 3)
        quantize("k", 0, 0, 2)
        quantize("q", 0, 0, 1)
        gram(0, 0, 1)
        gram(0, 1, 2)
        interleave(nc.scalar.copy, "q", 0, 1)
        keep_turned("v", 0, 0)
        interleave(nc.scalar.copy, "q", 1, 1)
        scale_v(1, 0)
        scale_v(1, 1)
        quantize("q", 0, 1, 2)
        gram(0, 2, 3)

        interleave_on_gpsimd("k", 1, 1)
        interleave_on_gpsimd("k", 1, 0)
        row_max(0, 0)
        gram(0, 3, 1)
        turn("v", 0, 1, 5)
        turn("v", 1, 0, 4)
        rest_of_softmax(0, (2, 3))

        interleave(nc.scalar.copy, "q", 1, 0)
        keep_turned("v", 0, 1)
        for h in range(2):
            keep_turned("pu", 0, h)
        for b in range(B):
            keep_gain(b)
        keep_turned("v", 1, 0)
        quantize("k", 1, 0, 2)
        quantize("q", 1, 0, 2)
        gram(1, 0, 1)
        gram(1, 1, 5)
        quantize("v", 0, 0, 2)
        quantize("pu", 0, 0, 2)

        row_max(1, 0)
        gram(1, 2, 6)
        gram(1, 3, 1)
        for t, number in enumerate((2, 3, 4, 7)):
            mix(0, t, number)
        rest_of_softmax(1, (5, 1))

        square(0, 0)
        inverse_root(0, 0)
        scale_v(1, 2)
        scale_v(1, 3)
        turn("v", 1, 1, 6)
        for h in range(2):
            keep_turned("pu", 1, h)
        square(0, 1)
        keep_turned("v", 1, 1)
        inverse_root(0, 1)
        quantize("v", 1, 0, 1)
        quantize("pu", 1, 0, 1)
        normalize(0, 0)
        shift1_bank = spread(2, shift1_cols, "shift1_bank")
        quantize("pu", 1, 1, 2)
        mix(1, 0, 5)
        mix(1, 1, 0)
        finish(nc.vector, 0, 0, shift0)
        quantize("v", 1, 1, 2)
        mix(1, 2, 6)
        mix(1, 3, 1)

        remaining = [(0, 2), (0, 3)] + [(1, t) for t in range(TILES)]
        square(*remaining[0])
        for done, following in zip(remaining, remaining[1:]):
            square(*following)
            inverse_root(*done)
        inverse_root(*remaining[-1])

        for t in (1, 2):
            normalize(0, t)
            finish(nc.gpsimd, 0, t, shift0)
        normalize(0, 3)
        normalize(1, 0)
        normalize(1, 1)
        finish(nc.vector, 1, 0, shift1_bank)
        finish(nc.gpsimd, 0, 3, shift0)
        for t in (2, 3):
            normalize(1, t)
            finish(nc.vector, 1, t - 1, shift1_bank)
        finish(nc.vector, 1, 3, shift1_bank)
